import numpy as np
import ml_dtypes


def mxq(x, axis, fmt="e4m3"):
    dtype, down = {"e4m3": (ml_dtypes.float8_e4m3fn, 7), "e5m2": (ml_dtypes.float8_e5m2, 14)}[fmt]
    v = np.moveaxis(np.asarray(x, np.float32).astype(ml_dtypes.bfloat16).astype(np.float64), axis, -1)
    blocks = v.reshape(v.shape[:-1] + (-1, 32))
    amax = np.abs(blocks).max(-1, keepdims=True)
    byte = np.maximum(np.where(amax > 0, np.frexp(amax)[1] - 1 + 127, 0) - down, 1)
    scale = np.exp2(byte - 127.0)
    codes = (blocks / scale).astype(np.float32).astype(dtype).astype(np.float64)
    return np.moveaxis((codes * scale).reshape(v.shape), -1, axis)


WIDE = False


def mx_kscale(k):
    if not WIDE:
        return np.ones(k)
    levels = np.array([10, -10, 5, -5, 0])
    if k % 512:
        return np.exp2(np.random.permutation(np.resize(levels, k // 32))).repeat(32)
    a = np.empty((k // 512, 16))
    for p in range(k // 512):
        a[p, :8] = np.random.permutation(np.resize(levels, 8))
        for g in range(8):
            far = levels[np.abs(levels - a[p, g]) >= 10]
            a[p, g + 8] = far[np.random.randint(len(far))]
    return np.exp2(a.ravel()).repeat(32)


def f64(x):
    return np.asarray(x).astype(np.float64)


def striped8(idx):
    return np.asarray(idx).reshape(8, -1, 16).transpose(0, 2, 1).reshape(128, -1).astype(np.uint16)


def unstriped8(offs):
    return offs.reshape(8, 16, -1).transpose(0, 2, 1).reshape(8, -1).astype(np.int64)


def pick8(x, idx, run):
    r = np.arange(len(x))
    return x[r[:, None], idx[r % (8 * run) // run]]


E2M1 = np.array([0.0, 0.5, 1.0, 1.5, 2.0, 3.0, 4.0, 6.0, -0.0, -0.5, -1.0, -1.5, -2.0, -3.0, -4.0, -6.0])


def pack_weight(w, fmt):
    k, n = w.shape
    w = f64(np.asarray(w, np.float32).astype(ml_dtypes.bfloat16)).reshape(k // 32, 32, n)
    amax = np.abs(w).max(1)
    if fmt == "e4m3":
        byte = np.frexp(amax)[1] - 1 + 127 - 7
    else:
        mant, ex = np.frexp(amax / 6.0)
        byte = np.where(mant > 0.5, ex, ex - 1) + 127
    byte = np.clip(np.where(amax > 0, byte, 1), 1, 254)
    scaled = (w * np.exp2(127.0 - byte)[:, None, :]).reshape(k, n).astype(np.float32)
    by_word = np.ascontiguousarray(scaled.reshape(k // 512, 128, 4, n).transpose(0, 1, 3, 2))
    if fmt == "e4m3":
        words = by_word.astype(ml_dtypes.float8_e4m3fn).view(np.uint8)
    else:
        c = by_word.astype(ml_dtypes.float4_e2m1fn).view(np.uint8) & 0xF
        words = (c[..., 0::2] | (c[..., 1::2] << 4)).reshape(k // 512, 128, 2 * n)
    return np.ascontiguousarray(words), np.ascontiguousarray(byte.astype(np.uint8).reshape(k // 512, 16, n))


def unpack_weight(words, scales, fmt):
    g, _, n = scales.shape
    words = np.ascontiguousarray(words).reshape(g, 128, n, -1)
    if fmt == "e4m3":
        vals = words.view(ml_dtypes.float8_e4m3fn).astype(np.float64)
    else:
        nib = np.empty((g, 128, n, 4), np.uint8)
        nib[..., 0::2] = words & 0xF
        nib[..., 1::2] = words >> 4
        vals = E2M1[nib]
    vals = vals * np.repeat(np.exp2(scales.astype(np.float64) - 127.0), 8, axis=1)[..., None]
    return vals.transpose(0, 1, 3, 2).reshape(g * 512, n)


D, V, Q, I = 512, 2048, 128, 512


def setup_inputs():
    n = np.random.standard_normal
    idx = np.stack([np.random.permutation(V)[:I] for _ in range(8)])
    fd = mx_kscale(D)
    vocp = pack_weight(n((D, V)) / fd[:, None], "e2m1")
    return {
        "hid": (n((D, Q)) * 1.0 / np.sqrt(D) * fd[:, None]).astype(np.float32),
        "voc_words": vocp[0],
        "voc_scales": vocp[1],
        "mult": (np.random.uniform(100.0, 300.0, (Q, 1))).astype(np.float32),
        "sw": (np.random.uniform(0.005, 0.02, (1, I))).astype(np.float32),
        "dhid": (n((D, Q)) * 1.0 / np.sqrt(D) * fd[:, None]).astype(np.float32),
        "base": (0.5 * n((Q, V))).astype(np.float32),
        "offs": striped8(idx),
    }


def reference(hid, voc_words, voc_scales, mult, sw, dhid, base, offs):
    idx = unstriped8(offs)
    vocu = unpack_weight(voc_words, voc_scales, "e2m1")
    hidq = mxq(f64(hid), 0, "e4m3")
    a = hidq.T @ vocu
    dhidq = mxq(f64(dhid), 0, "e4m3")
    ta = dhidq.T @ vocu
    m1 = np.max(a, axis=1, keepdims=True)
    p = np.exp(a - m1)
    z = np.sum(p, axis=1, keepdims=True)
    px = np.exp(pick8(a, idx, 16) - m1)
    u1 = px / z
    du1 = f64(sw) * (1.0 - u1 * f64(mult)) / u1 + f64(sw) * np.log(u1) * (-1.0) * f64(mult)
    dpx = du1 / z
    dz = np.sum(du1 * px / np.square(z) * (-1.0), axis=1, keepdims=True)
    xp = ta * p
    xz = np.sum(xp, axis=1, keepdims=True)
    xpx = pick8(ta, idx, 16) * px
    xu1 = (xpx - xz * px / z) / z
    xdu1 = (xu1 * f64(mult) * (-1.0) * f64(sw) - xu1 * f64(sw) * (1.0 - u1 * f64(mult)) / u1) / u1 + xu1 / u1 * f64(sw) * (-1.0) * f64(mult)
    xdpx = (xdu1 - xz * du1 / z) / z
    xdz = np.sum((xdu1 * px + xpx * du1 - xz * z * 2.0 * du1 * px / np.square(z)) / np.square(z) * (-1.0), axis=1, keepdims=True)
    xe1 = xdpx * px + xpx * dpx
    xs1 = np.zeros((Q, V))
    xs1[np.arange(Q)[:, None], idx[np.arange(Q) % 128 // 16]] = xe1
    xda = xdz * p + xp * dz + xs1
    y = xda * 64.0 + f64(base)
    return y

@@ -1,0 +1,235 @@
+from contextlib import ExitStack
+
+import concourse.mybir as mybir
+from concourse.masks import make_identity
+
+F32 = mybir.dt.float32
+BF16 = mybir.dt.bfloat16
+I32 = mybir.dt.int32
+U32 = mybir.dt.uint32
+U16 = mybir.dt.uint16
+U8 = mybir.dt.uint8
+FP8X4 = mybir.dt.float8_e4m3fn_x4
+FP4X4 = mybir.dt.float4_e2m1fn_x4
+ALU = mybir.AluOpType
+ACT = mybir.ActivationFunctionType
+AX = mybir.AxisListType
+
+P = 128
+D, V, Q, SLOTS = 512, 2048, 128, 512
+BANK = 512
+GROUPS = V // BANK
+HALF = V // 2
+MODES = ("Z","X","X","X")
+FLOPS = 2 * 2 * D * V * Q
+
+
+def tile_attend_hvfocal_heads_kernel(tc, hid, voc_words, voc_scales, mult, sw, dhid, base, offs, out):
+    nc = tc.nc
+    with ExitStack() as ctx:
+        sb = ctx.enter_context(tc.tile_pool(name="sb", bufs=1))
+        ps = ctx.enter_context(tc.psum_pool(name="ps", bufs=1))
+
+        def col(name):
+            return sb.tile([P, 1], F32, name=name)
+
+        def bank(b, name):
+            return ps.tile([P, BANK], F32, name=name, tag="bank%d" % b)
+
+        offsets = sb.tile([P, SLOTS // 16], U16, name="offsets")
+        voc_sc = sb.tile([P, V], U8, name="voc_sc", align_bytes=64)
+        xs = sb.tile([P, V], F32, name="xs")
+        minus_two = col("minus_two")
+        nc.vector.memset(voc_sc[:].bitcast(I32), 0)
+        nc.vector.memset(minus_two[:], -2.0)
+        nc.vector.memset(xs[:], 0.0)
+        ident = sb.tile([P, P], F32, name="ident")
+        make_identity(nc, ident[:])
+        exp_m2 = col("exp_m2")
+        nc.scalar.activation(exp_m2[:], minus_two[:], ACT.Exp)
+
+        hid_raw = sb.tile([P, 4, Q], F32, name="hid_raw")
+        dhid_raw = sb.tile([P, 4, Q], F32, name="dhid_raw")
+        words = [sb.tile([P, V], U8, name="words%d" % h, align_bytes=64) for h in range(2)]
+        sw_cols = sb.tile([P, 4], F32, name="sw_cols")
+        mult_col = col("mult_col")
+        base_sb = [sb.tile([P, HALF], F32, name="base%d" % h) for h in range(2)]
+
+        nc.sync.dma_start(hid_raw[:], hid.rearrange("(p j) q -> p j q", j=4))
+        for quad in range(4):
+            nc.sync.dma_start(
+                voc_sc[32 * quad : 32 * quad + 4, :].bitcast(I32),
+                voc_scales[0, 4 * quad : 4 * quad + 4, :].bitcast(I32),
+            )
+        nc.sync.dma_start(words[0][:].bitcast(I32), voc_words[0, :, 0:V].bitcast(I32))
+        nc.sync.dma_start(dhid_raw[:], dhid.rearrange("(p j) q -> p j q", j=4))
+        nc.sync.dma_start(sw_cols[:], sw.rearrange("o (p c) -> (o p) c", c=4))
+        nc.sync.dma_start(words[1][:].bitcast(I32), voc_words[0, :, V : 2 * V].bitcast(I32))
+        nc.sync.dma_start(offsets[:], offs)
+        nc.sync.dma_start(mult_col[:], mult)
+        for h in range(2):
+            nc.sync.dma_start(base_sb[h][:], base[:, h * HALF : (h + 1) * HALF])
+
+        codes, scales = [], []
+        for name, raw, cast in (("hid", hid_raw, nc.vector.tensor_copy), ("dhid", dhid_raw, nc.scalar.copy)):
+            grouped = sb.tile([P, Q, 4], BF16, name=name + "_grouped", align_bytes=64)
+            cast(
+                grouped[:].rearrange("p (c i) t -> p c t i", i=4),
+                raw[:].rearrange("p t (c i) -> p c t i", i=4),
+            )
+            cd = sb.tile([P, Q], U32, name=name + "_codes", align_bytes=64)
+            sc = sb.tile([P, Q], U8, name=name + "_scales", align_bytes=64)
+            nc.vector.quantize_mx(out=cd[:].bitcast(FP8X4), scales=sc[:], in_=grouped[:].rearrange("p q t -> p (q t)"))
+            codes.append(cd)
+            scales.append(sc)
+
+        sw_ps = bank(7, "sw_ps")
+        for c in range(4):
+            nc.tensor.transpose(sw_ps[:, c * P : (c + 1) * P], sw_cols[:, c : c + 1].to_broadcast([P, P]), ident[:])
+        s64 = sb.tile([P, SLOTS], F32, name="s64")
+        s64_sum = col("s64_sum")
+        nc.scalar.activation(
+            s64[:].rearrange("p (n c) -> p n c", c=4),
+            sw_ps[:].rearrange("p (c n) -> p n c", c=4),
+            ACT.Copy,
+            scale=64.0,
+            accum_out=s64_sum[:],
+        )
+
+        a = sb.tile([P, V], F32, name="a")
+        ta = sb.tile([P, V], F32, name="ta")
+        group_max = sb.tile([P, GROUPS], F32, name="group_max")
+
+        def score(side, g):
+            acc = bank(4 * side + g, "score%d_%d" % (side, g))
+            h, c0 = divmod(g * BANK, HALF)
+            nc.tensor.matmul_mx(
+                out=acc[:],
+                lhsT=codes[side][:].bitcast(FP8X4),
+                lhsT_scale=scales[side][:],
+                rhs=words[h][:, 2 * c0 : 2 * (c0 + BANK)].bitcast(FP4X4),
+                rhs_scale=voc_sc[:, g * BANK : (g + 1) * BANK],
+                start=True,
+                stop=True,
+            )
+            cols = slice(g * BANK, (g + 1) * BANK)
+            if side == 0:
+                nc.vector.tensor_scalar(a[:, cols], acc[:], 1.0, None, ALU.mult, ALU.max, accum_out=group_max[:, g : g + 1])
+            else:
+                nc.scalar.copy(ta[:, cols], acc[:])
+
+        score(0, 0)
+        for g in range(1, GROUPS):
+            score(0, g)
+            score(1, g - 1)
+        score(1, GROUPS - 1)
+
+        neg_max = col("neg_max")
+        nc.vector.tensor_reduce(neg_max[:], group_max[:], AX.X, ALU.max, negate=True)
+        a_listed = sb.tile([P, SLOTS], F32, name="a_listed")
+        ta_listed = sb.tile([P, SLOTS], F32, name="ta_listed")
+        nc.vector.tensor_copy(a_listed[:], a[:].indirect(offsets[:]))
+        nc.vector.tensor_copy(ta_listed[:], ta[:].indirect(offsets[:]))
+
+        p = [sb.tile([P, HALF], F32, name="p%d" % h) for h in range(2)]
+        xp = [sb.tile([P, HALF], F32, name="xp%d" % h) for h in range(2)]
+        z_half = [col("z_half%d" % h) for h in range(2)]
+        xz_half = [col("xz_half%d" % h) for h in range(2)]
+        for h in range(2):
+            cols = slice(h * HALF, (h + 1) * HALF)
+            nc.scalar.activation(p[h][:], a[:, cols], ACT.Exp, bias=neg_max[:], accum_out=z_half[h][:])
+        px = sb.tile([P, SLOTS], F32, name="px")
+        nc.scalar.activation(px[:], a_listed[:], ACT.Exp, bias=neg_max[:])
+        nc.vector.scalar_tensor_tensor(xp[0][:], ta[:, 0:HALF], 1.0, p[0][:], ALU.mult, ALU.mult, accum_out=xz_half[0][:])
+        z = col("z")
+        nc.vector.tensor_tensor(z[:], z_half[0][:], z_half[1][:], ALU.add)
+        nc.vector.scalar_tensor_tensor(xp[1][:], ta[:, HALF:V], 1.0, p[1][:], ALU.mult, ALU.mult, accum_out=xz_half[1][:])
+        neg_z = col("neg_z")
+        neg_rz = col("neg_rz")
+        kappa = col("kappa")
+        neg_tbar = col("neg_tbar")
+        nc.vector.tensor_scalar(neg_z[:], z_half[0][:], z_half[1][:], -1.0, ALU.add, ALU.mult)
+        nc.vector.reciprocal(neg_rz[:], neg_z[:])
+        nc.vector.tensor_tensor(kappa[:], neg_rz[:], mult_col[:], ALU.mult)
+        nc.vector.tensor_scalar(neg_tbar[:], xz_half[0][:], xz_half[1][:], neg_rz[:], ALU.add, ALU.mult)
+
+        lnz_m2 = col("lnz_m2")
+        beta = col("beta")
+        nc.scalar.activation(lnz_m2[:], z[:], ACT.Ln, scale=exp_m2[:])
+        nc.scalar.activation(beta[:], lnz_m2[:], ACT.Identity, scale=-1.0, bias=neg_max[:])
+
+        su = sb.tile([P, SLOTS], F32, name="su")
+        w = sb.tile([P, SLOTS], F32, name="w")
+        xe = sb.tile([P, SLOTS], F32, name="xe")
+        su_sum, w_sum, xe_sum = col("su_sum"), col("w_sum"), col("xe_sum")
+        nc.vector.scalar_tensor_tensor(su[:], px[:], kappa[:], s64[:], ALU.mult, ALU.mult, accum_out=su_sum[:])
+        nc.vector.scalar_tensor_tensor(w[:], a_listed[:], beta[:], su[:], ALU.add, ALU.mult, accum_out=w_sum[:])
+        nc.vector.scalar_tensor_tensor(xe[:], ta_listed[:], neg_tbar[:], w[:], ALU.add, ALU.mult, accum_out=xe_sum[:])
+        nc.vector.tensor_copy(xs[:].indirect(offsets[:]), xe[:])
+
+        g_rest, dz_rest, dz64, dz_tbar, xdz64 = col("g_rest"), col("dz_rest"), col("dz64"), col("dz_tbar"), col("xdz64")
+        nc.scalar.activation(g_rest[:], su_sum[:], ACT.Identity, scale=-1.0, bias=s64_sum[:])
+        nc.scalar.activation(dz_rest[:], g_rest[:], ACT.Copy, scale=neg_rz[:])
+        nc.scalar.activation(dz64[:], w_sum[:], ACT.Identity, scale=neg_rz[:], bias=dz_rest[:])
+        nc.scalar.activation(dz_tbar[:], dz64[:], ACT.Copy, scale=neg_tbar[:])
+        nc.scalar.activation(xdz64[:], xe_sum[:], ACT.Identity, scale=neg_rz[:], bias=dz_tbar[:])
+
+        def part(tiles, g):
+            h, c0 = divmod(g * BANK, HALF)
+            return tiles[h][:, c0 : c0 + BANK]
+
+        def turn_add(acc, src, start, stop):
+            for j in range(4):
+                blk = slice(j * P, (j + 1) * P)
+                nc.tensor.matmul(acc[:, blk], src[:, blk], ident[:], start=start and j == 0, stop=stop and j == 3, is_transpose=True)
+
+        turned = {}
+        back = {}
+
+        def pe_first(g):
+            acc = bank(g, "turned%d" % g)
+            turn_add(acc, part(base_sb, g), True, False)
+            if MODES[g] == "X":
+                t1 = sb.tile([P, BANK], F32, name="xp_dz%d" % g)
+                nc.scalar.activation(t1[:], part(xp, g), ACT.Copy, scale=dz64[:])
+                turn_add(acc, t1[:], False, False)
+            t2 = sb.tile([P, BANK], F32, name="p_xdz%d" % g)
+            nc.scalar.activation(t2[:], part(p, g), ACT.Copy, scale=xdz64[:])
+            turn_add(acc, t2[:], False, True)
+            turned[g] = acc
+
+        def pe_second(g):
+            t3 = sb.tile([P, BANK], F32, name="turned_sb%d" % g)
+            nc.scalar.copy(t3[:], turned[g][:])
+            acc = bank(4 + g, "back%d" % g)
+            for j in range(4):
+                blk = slice(j * P, (j + 1) * P)
+                nc.tensor.transpose(acc[:, blk], t3[:, blk], ident[:])
+            back[g] = acc
+
+        def finish(g):
+            cols = slice(g * BANK, (g + 1) * BANK)
+            res = sb.tile([P, BANK], F32, name="res%d" % g)
+            if MODES[g] == "Z":
+                r1 = sb.tile([P, BANK], F32, name="r1_%d" % g)
+                r2 = sb.tile([P, BANK], F32, name="r2_%d" % g)
+                nc.vector.scalar_tensor_tensor(r1[:], part(xp, g), dz64[:], part(base_sb, g), ALU.mult, ALU.add)
+                nc.vector.scalar_tensor_tensor(r2[:], part(p, g), xdz64[:], r1[:], ALU.mult, ALU.add)
+                nc.vector.tensor_tensor(res[:], r2[:], xs[:, cols], ALU.add)
+            elif MODES[g] == "Y":
+                r1 = sb.tile([P, BANK], F32, name="r1_%d" % g)
+                nc.vector.scalar_tensor_tensor(r1[:], part(xp, g), dz64[:], xs[:, cols], ALU.mult, ALU.add)
+                nc.vector.tensor_tensor(res[:], back[g][:], r1[:], ALU.add)
+            else:
+                nc.vector.tensor_tensor(res[:], back[g][:], xs[:, cols], ALU.add)
+            nc.sync.dma_start(out[:, cols], res[:])
+
+        pe_groups = [g for g in range(GROUPS) if MODES[g] != "Z"]
+        for k, g in enumerate(pe_groups):
+            pe_first(g)
+            if k > 0:
+                pe_second(pe_groups[k - 1])
+        if pe_groups:
+            pe_second(pe_groups[-1])
+        for g in range(GROUPS):
+            finish(g)

@@ -20,7 +20,7 @@ D, V, Q, SLOTS = 512, 2048, 128, 512
 BANK = 512
 GROUPS = V // BANK
 HALF = V // 2
-MODES = ("Z","X","X","X")
+MODES = ("Z","Z","Z","Z")
 FLOPS = 2 * 2 * D * V * Q
 
 
@@ -39,7 +39,7 @@ def tile_attend_hvfocal_heads_kernel(tc, hid, voc_words, voc_scales, mult, sw, d
         offsets = sb.tile([P, SLOTS // 16], U16, name="offsets")
         voc_sc = sb.tile([P, V], U8, name="voc_sc", align_bytes=64)
         xs = sb.tile([P, V], F32, name="xs")
-        minus_two = col("minus_two")
+        minus_two = sb.tile([P, 1], F32, name="minus_two", tag="small0")
         nc.vector.memset(voc_sc[:].bitcast(I32), 0)
         nc.vector.memset(minus_two[:], -2.0)
         nc.vector.memset(xs[:], 0.0)
@@ -48,12 +48,9 @@ def tile_attend_hvfocal_heads_kernel(tc, hid, voc_words, voc_scales, mult, sw, d
         exp_m2 = col("exp_m2")
         nc.scalar.activation(exp_m2[:], minus_two[:], ACT.Exp)
 
-        hid_raw = sb.tile([P, 4, Q], F32, name="hid_raw")
-        dhid_raw = sb.tile([P, 4, Q], F32, name="dhid_raw")
+        hid_raw = sb.tile([P, 4, Q], F32, name="hid_raw", tag="raw0")
+        dhid_raw = sb.tile([P, 4, Q], F32, name="dhid_raw", tag="raw1")
         words = [sb.tile([P, V], U8, name="words%d" % h, align_bytes=64) for h in range(2)]
-        sw_cols = sb.tile([P, 4], F32, name="sw_cols")
-        mult_col = col("mult_col")
-        base_sb = [sb.tile([P, HALF], F32, name="base%d" % h) for h in range(2)]
 
         nc.sync.dma_start(hid_raw[:], hid.rearrange("(p j) q -> p j q", j=4))
         for quad in range(4):
@@ -63,12 +60,10 @@ def tile_attend_hvfocal_heads_kernel(tc, hid, voc_words, voc_scales, mult, sw, d
             )
         nc.sync.dma_start(words[0][:].bitcast(I32), voc_words[0, :, 0:V].bitcast(I32))
         nc.sync.dma_start(dhid_raw[:], dhid.rearrange("(p j) q -> p j q", j=4))
-        nc.sync.dma_start(sw_cols[:], sw.rearrange("o (p c) -> (o p) c", c=4))
         nc.sync.dma_start(words[1][:].bitcast(I32), voc_words[0, :, V : 2 * V].bitcast(I32))
         nc.sync.dma_start(offsets[:], offs)
-        nc.sync.dma_start(mult_col[:], mult)
-        for h in range(2):
-            nc.sync.dma_start(base_sb[h][:], base[:, h * HALF : (h + 1) * HALF])
+        sw_cols = sb.tile([P, 4], F32, name="sw_cols", tag="small0")
+        nc.sync.dma_start(sw_cols[:], sw.rearrange("o (p c) -> (o p) c", c=4))
 
         codes, scales = [], []
         for name, raw, cast in (("hid", hid_raw, nc.vector.tensor_copy), ("dhid", dhid_raw, nc.scalar.copy)):
@@ -83,18 +78,11 @@ def tile_attend_hvfocal_heads_kernel(tc, hid, voc_words, voc_scales, mult, sw, d
             codes.append(cd)
             scales.append(sc)
 
-        sw_ps = bank(7, "sw_ps")
-        for c in range(4):
-            nc.tensor.transpose(sw_ps[:, c * P : (c + 1) * P], sw_cols[:, c : c + 1].to_broadcast([P, P]), ident[:])
-        s64 = sb.tile([P, SLOTS], F32, name="s64")
-        s64_sum = col("s64_sum")
-        nc.scalar.activation(
-            s64[:].rearrange("p (n c) -> p n c", c=4),
-            sw_ps[:].rearrange("p (c n) -> p n c", c=4),
-            ACT.Copy,
-            scale=64.0,
-            accum_out=s64_sum[:],
-        )
+        mult_col = sb.tile([P, 1], F32, name="mult_col", tag="hid_grouped", align_bytes=64)
+        nc.sync.dma_start(mult_col[:], mult)
+        base_sb = [sb.tile([P, HALF], F32, name="base%d" % h, tag="raw%d" % h) for h in range(2)]
+        for h in range(2):
+            nc.sync.dma_start(base_sb[h][:], base[:, h * HALF : (h + 1) * HALF])
 
         a = sb.tile([P, V], F32, name="a")
         ta = sb.tile([P, V], F32, name="ta")
@@ -118,11 +106,16 @@ def tile_attend_hvfocal_heads_kernel(tc, hid, voc_words, voc_scales, mult, sw, d
             else:
                 nc.scalar.copy(ta[:, cols], acc[:])
 
-        score(0, 0)
-        for g in range(1, GROUPS):
+        for g in range(GROUPS):
             score(0, g)
-            score(1, g - 1)
-        score(1, GROUPS - 1)
+            score(1, g)
+
+        sw_ps = bank(0, "sw_ps")
+        sw_sum_ps = bank(1, "sw_sum_ps")
+        for c in range(4):
+            spread = sw_cols[:, c : c + 1].to_broadcast([P, P])
+            nc.tensor.transpose(sw_ps[:, c * P : (c + 1) * P], spread, ident[:])
+            nc.tensor.matmul(sw_sum_ps[:, 0:P], spread, ident[:], start=c == 0, stop=c == 3, is_transpose=True)
 
         neg_max = col("neg_max")
         nc.vector.tensor_reduce(neg_max[:], group_max[:], AX.X, ALU.max, negate=True)
@@ -135,44 +128,53 @@ def tile_attend_hvfocal_heads_kernel(tc, hid, voc_words, voc_scales, mult, sw, d
         xp = [sb.tile([P, HALF], F32, name="xp%d" % h) for h in range(2)]
         z_half = [col("z_half%d" % h) for h in range(2)]
         xz_half = [col("xz_half%d" % h) for h in range(2)]
-        for h in range(2):
-            cols = slice(h * HALF, (h + 1) * HALF)
-            nc.scalar.activation(p[h][:], a[:, cols], ACT.Exp, bias=neg_max[:], accum_out=z_half[h][:])
         px = sb.tile([P, SLOTS], F32, name="px")
+        nc.scalar.activation(p[0][:], a[:, 0:HALF], ACT.Exp, bias=neg_max[:], accum_out=z_half[0][:])
         nc.scalar.activation(px[:], a_listed[:], ACT.Exp, bias=neg_max[:])
-        nc.vector.scalar_tensor_tensor(xp[0][:], ta[:, 0:HALF], 1.0, p[0][:], ALU.mult, ALU.mult, accum_out=xz_half[0][:])
-        z = col("z")
-        nc.vector.tensor_tensor(z[:], z_half[0][:], z_half[1][:], ALU.add)
-        nc.vector.scalar_tensor_tensor(xp[1][:], ta[:, HALF:V], 1.0, p[1][:], ALU.mult, ALU.mult, accum_out=xz_half[1][:])
-        neg_z = col("neg_z")
-        neg_rz = col("neg_rz")
-        kappa = col("kappa")
-        neg_tbar = col("neg_tbar")
-        nc.vector.tensor_scalar(neg_z[:], z_half[0][:], z_half[1][:], -1.0, ALU.add, ALU.mult)
-        nc.vector.reciprocal(neg_rz[:], neg_z[:])
-        nc.vector.tensor_tensor(kappa[:], neg_rz[:], mult_col[:], ALU.mult)
-        nc.vector.tensor_scalar(neg_tbar[:], xz_half[0][:], xz_half[1][:], neg_rz[:], ALU.add, ALU.mult)
-
+        nc.scalar.activation(p[1][:], a[:, HALF:V], ACT.Exp, bias=neg_max[:], accum_out=z_half[1][:])
+        z, rz, tbar = col("z"), col("rz"), col("tbar")
+        nc.scalar.activation(z[:], z_half[0][:], ACT.Identity, bias=z_half[1][:])
         lnz_m2 = col("lnz_m2")
         beta = col("beta")
         nc.scalar.activation(lnz_m2[:], z[:], ACT.Ln, scale=exp_m2[:])
         nc.scalar.activation(beta[:], lnz_m2[:], ACT.Identity, scale=-1.0, bias=neg_max[:])
 
+        nc.vector.scalar_tensor_tensor(xp[0][:], ta[:, 0:HALF], 1.0, p[0][:], ALU.mult, ALU.mult, accum_out=xz_half[0][:])
         su = sb.tile([P, SLOTS], F32, name="su")
         w = sb.tile([P, SLOTS], F32, name="w")
         xe = sb.tile([P, SLOTS], F32, name="xe")
         su_sum, w_sum, xe_sum = col("su_sum"), col("w_sum"), col("xe_sum")
-        nc.vector.scalar_tensor_tensor(su[:], px[:], kappa[:], s64[:], ALU.mult, ALU.mult, accum_out=su_sum[:])
+        nc.vector.scalar_tensor_tensor(
+            su[:].rearrange("p (n c) -> p n c", c=4),
+            px[:].rearrange("p (n c) -> p n c", c=4),
+            mult_col[:],
+            sw_ps[:].rearrange("p (c n) -> p n c", c=4),
+            ALU.mult,
+            ALU.mult,
+            accum_out=su_sum[:],
+        )
+        nc.vector.reciprocal(rz[:], z[:])
+        nc.vector.scalar_tensor_tensor(xp[1][:], ta[:, HALF:V], 1.0, p[1][:], ALU.mult, ALU.mult, accum_out=xz_half[1][:])
+        neg_rz, q2, neg_q2 = col("neg_rz"), col("q2"), col("neg_q2")
+        nc.scalar.activation(neg_rz[:], rz[:], ACT.Copy, scale=-64.0)
+        nc.scalar.activation(q2[:], rz[:], ACT.Square, scale=8.0)
+        nc.scalar.activation(neg_q2[:], q2[:], ACT.Copy, scale=-1.0)
+        sw_quads = sb.tile([P, P], F32, name="sw_quads")
+        s64_sum = col("s64_sum")
+        nc.scalar.activation(sw_quads[:], sw_sum_ps[:, 0:P], ACT.Copy, scale=neg_rz[:], accum_out=s64_sum[:])
+
+        nc.vector.tensor_scalar(tbar[:], xz_half[0][:], xz_half[1][:], rz[:], ALU.add, ALU.mult)
         nc.vector.scalar_tensor_tensor(w[:], a_listed[:], beta[:], su[:], ALU.add, ALU.mult, accum_out=w_sum[:])
-        nc.vector.scalar_tensor_tensor(xe[:], ta_listed[:], neg_tbar[:], w[:], ALU.add, ALU.mult, accum_out=xe_sum[:])
+        nc.vector.scalar_tensor_tensor(xe[:], ta_listed[:], tbar[:], w[:], ALU.subtract, ALU.mult, accum_out=xe_sum[:])
         nc.vector.tensor_copy(xs[:].indirect(offsets[:]), xe[:])
 
-        g_rest, dz_rest, dz64, dz_tbar, xdz64 = col("g_rest"), col("dz_rest"), col("dz64"), col("dz_tbar"), col("xdz64")
-        nc.scalar.activation(g_rest[:], su_sum[:], ACT.Identity, scale=-1.0, bias=s64_sum[:])
-        nc.scalar.activation(dz_rest[:], g_rest[:], ACT.Copy, scale=neg_rz[:])
-        nc.scalar.activation(dz64[:], w_sum[:], ACT.Identity, scale=neg_rz[:], bias=dz_rest[:])
+        neg_tbar = col("neg_tbar")
+        nc.scalar.activation(neg_tbar[:], tbar[:], ACT.Copy, scale=-1.0)
+        dz_rest, dz64, dz_tbar, xdz64 = col("dz_rest"), col("dz64"), col("dz_tbar"), col("xdz64")
+        nc.scalar.activation(dz_rest[:], su_sum[:], ACT.Identity, scale=neg_q2[:], bias=s64_sum[:])
+        nc.scalar.activation(dz64[:], w_sum[:], ACT.Identity, scale=q2[:], bias=dz_rest[:])
         nc.scalar.activation(dz_tbar[:], dz64[:], ACT.Copy, scale=neg_tbar[:])
-        nc.scalar.activation(xdz64[:], xe_sum[:], ACT.Identity, scale=neg_rz[:], bias=dz_tbar[:])
+        nc.scalar.activation(xdz64[:], xe_sum[:], ACT.Identity, scale=q2[:], bias=dz_tbar[:])
 
         def part(tiles, g):
             h, c0 = divmod(g * BANK, HALF)
@@ -184,6 +186,19 @@ def tile_attend_hvfocal_heads_kernel(tc, hid, voc_words, voc_scales, mult, sw, d
                 nc.tensor.matmul(acc[:, blk], src[:, blk], ident[:], start=start and j == 0, stop=stop and j == 3, is_transpose=True)
 
         turned = {}
+        lin = {}
+        pooled = {}
+
+        def linear(g):
+            lin[g] = sb.tile([P, BANK], F32, name="lin%d" % g)
+            nc.scalar.activation(lin[g][:], ta[:, g * BANK : (g + 1) * BANK], ACT.Identity, scale=dz64[:], bias=xdz64[:])
+
+        def pool_group(g):
+            q1 = sb.tile([P, BANK], F32, name="q1_%d" % g)
+            pooled[g] = sb.tile([P, BANK], F32, name="pooled%d" % g)
+            nc.gpsimd.tensor_tensor(q1[:], lin[g][:], part(p, g), ALU.mult)
+            nc.gpsimd.tensor_tensor(pooled[g][:], q1[:], part(base_sb, g), ALU.add)
+
         back = {}
 
         def pe_first(g):
@@ -194,7 +209,10 @@ def tile_attend_hvfocal_heads_kernel(tc, hid, voc_words, voc_scales, mult, sw, d
                 nc.scalar.activation(t1[:], part(xp, g), ACT.Copy, scale=dz64[:])
                 turn_add(acc, t1[:], False, False)
             t2 = sb.tile([P, BANK], F32, name="p_xdz%d" % g)
-            nc.scalar.activation(t2[:], part(p, g), ACT.Copy, scale=xdz64[:])
+            if MODES[g] == "U":
+                nc.gpsimd.tensor_tensor(t2[:], lin[g][:], part(p, g), ALU.mult)
+            else:
+                nc.scalar.activation(t2[:], part(p, g), ACT.Copy, scale=xdz64[:])
             turn_add(acc, t2[:], False, True)
             turned[g] = acc
 
@@ -215,16 +233,24 @@ def tile_attend_hvfocal_heads_kernel(tc, hid, voc_words, voc_scales, mult, sw, d
                 r2 = sb.tile([P, BANK], F32, name="r2_%d" % g)
                 nc.vector.scalar_tensor_tensor(r1[:], part(xp, g), dz64[:], part(base_sb, g), ALU.mult, ALU.add)
                 nc.vector.scalar_tensor_tensor(r2[:], part(p, g), xdz64[:], r1[:], ALU.mult, ALU.add)
-                nc.vector.tensor_tensor(res[:], r2[:], xs[:, cols], ALU.add)
+                nc.vector.scalar_tensor_tensor(res[:], xs[:, cols], neg_rz[:], r2[:], ALU.mult, ALU.add)
+            elif MODES[g] == "W":
+                nc.vector.scalar_tensor_tensor(res[:], xs[:, cols], neg_rz[:], pooled[g][:], ALU.mult, ALU.add)
             elif MODES[g] == "Y":
                 r1 = sb.tile([P, BANK], F32, name="r1_%d" % g)
-                nc.vector.scalar_tensor_tensor(r1[:], part(xp, g), dz64[:], xs[:, cols], ALU.mult, ALU.add)
-                nc.vector.tensor_tensor(res[:], back[g][:], r1[:], ALU.add)
+                nc.vector.scalar_tensor_tensor(r1[:], part(xp, g), dz64[:], back[g][:], ALU.mult, ALU.add)
+                nc.vector.scalar_tensor_tensor(res[:], xs[:, cols], neg_rz[:], r1[:], ALU.mult, ALU.add)
             else:
-                nc.vector.tensor_tensor(res[:], back[g][:], xs[:, cols], ALU.add)
+                nc.vector.scalar_tensor_tensor(res[:], xs[:, cols], neg_rz[:], back[g][:], ALU.mult, ALU.add)
             nc.sync.dma_start(out[:, cols], res[:])
 
-        pe_groups = [g for g in range(GROUPS) if MODES[g] != "Z"]
+        for g in range(GROUPS):
+            if MODES[g] in ("W", "U"):
+                linear(g)
+        for g in range(GROUPS):
+            if MODES[g] == "W":
+                pool_group(g)
+        pe_groups = [g for g in range(GROUPS) if MODES[g] in ("X", "Y", "U")]
         for k, g in enumerate(pe_groups):
             pe_first(g)
             if k > 0:

@@ -13,14 +13,22 @@ FP8X4 = mybir.dt.float8_e4m3fn_x4
 FP4X4 = mybir.dt.float4_e2m1fn_x4
 ALU = mybir.AluOpType
 ACT = mybir.ActivationFunctionType
-AX = mybir.AxisListType
+AXIS = mybir.AxisListType
 
 P = 128
+PACK = 4
 D, V, Q, SLOTS = 512, 2048, 128, 512
-BANK = 512
-GROUPS = V // BANK
+GROUP = 512
+GROUPS = V // GROUP
 HALF = V // 2
-MODES = ("Z","Z","Z","Z")
+BLOCKS = [slice(j * P, (j + 1) * P) for j in range(GROUP // P)]
+GROUP_HALVES = [slice(0, GROUP // 2), slice(GROUP // 2, GROUP)]
+OUT_SCALE = 64.0
+
+GPSIMD_GROUP = 0
+VECTOR_GROUP = 1
+TENSOR_GROUPS = (2, 3)
+
 FLOPS = 2 * 2 * D * V * Q
 
 
@@ -30,53 +38,70 @@ def tile_attend_hvfocal_heads_kernel(tc, hid, voc_words, voc_scales, mult, sw, d
         sb = ctx.enter_context(tc.tile_pool(name="sb", bufs=1))
         ps = ctx.enter_context(tc.psum_pool(name="ps", bufs=1))
 
-        def col(name):
+        def column(name):
             return sb.tile([P, 1], F32, name=name)
 
+        def slot_tile(name):
+            return sb.tile([P, SLOTS], F32, name=name)
+
+        def group_tile(name, tag=None):
+            return sb.tile([P, GROUP], F32, name=name, tag=tag or name)
+
         def bank(b, name):
-            return ps.tile([P, BANK], F32, name=name, tag="bank%d" % b)
+            return ps.tile([P, GROUP], F32, name=name, tag="bank%d" % b)
+
+        def group_cols(g):
+            return slice(g * GROUP, (g + 1) * GROUP)
+
+        def group_of(halves, g):
+            h, c0 = divmod(g * GROUP, HALF)
+            return halves[h][:, c0 : c0 + GROUP]
 
         offsets = sb.tile([P, SLOTS // 16], U16, name="offsets")
         voc_sc = sb.tile([P, V], U8, name="voc_sc", align_bytes=64)
-        xs = sb.tile([P, V], F32, name="xs")
-        minus_two = sb.tile([P, 1], F32, name="minus_two", tag="small0")
+        scattered = sb.tile([P, V], F32, name="scattered")
+        minus_two = sb.tile([P, 1], F32, name="minus_two", tag="small")
         nc.vector.memset(voc_sc[:].bitcast(I32), 0)
         nc.vector.memset(minus_two[:], -2.0)
-        nc.vector.memset(xs[:], 0.0)
+        nc.vector.memset(scattered[:], 0.0)
         ident = sb.tile([P, P], F32, name="ident")
         make_identity(nc, ident[:])
-        exp_m2 = col("exp_m2")
+        exp_m2 = column("exp_m2")
         nc.scalar.activation(exp_m2[:], minus_two[:], ACT.Exp)
 
-        hid_raw = sb.tile([P, 4, Q], F32, name="hid_raw", tag="raw0")
-        dhid_raw = sb.tile([P, 4, Q], F32, name="dhid_raw", tag="raw1")
-        words = [sb.tile([P, V], U8, name="words%d" % h, align_bytes=64) for h in range(2)]
-
-        nc.sync.dma_start(hid_raw[:], hid.rearrange("(p j) q -> p j q", j=4))
+        hid_raw = sb.tile([P, PACK, Q], F32, name="hid_raw", tag="raw0")
+        dhid_raw = sb.tile([P, PACK, Q], F32, name="dhid_raw", tag="raw1")
+        words_head = sb.tile([P, 2 * GROUP], U8, name="words_head", align_bytes=64)
+        words_rest = sb.tile([P, 2 * (V - GROUP)], U8, name="words_rest", align_bytes=64)
+        nc.sync.dma_start(hid_raw[:], hid.rearrange("(p t) q -> p t q", t=PACK))
         for quad in range(4):
             nc.sync.dma_start(
                 voc_sc[32 * quad : 32 * quad + 4, :].bitcast(I32),
                 voc_scales[0, 4 * quad : 4 * quad + 4, :].bitcast(I32),
             )
-        nc.sync.dma_start(words[0][:].bitcast(I32), voc_words[0, :, 0:V].bitcast(I32))
-        nc.sync.dma_start(dhid_raw[:], dhid.rearrange("(p j) q -> p j q", j=4))
-        nc.sync.dma_start(words[1][:].bitcast(I32), voc_words[0, :, V : 2 * V].bitcast(I32))
+        nc.sync.dma_start(words_head[:].bitcast(I32), voc_words[0, :, 0 : 2 * GROUP].bitcast(I32))
+        nc.sync.dma_start(dhid_raw[:], dhid.rearrange("(p t) q -> p t q", t=PACK))
+        nc.sync.dma_start(words_rest[:].bitcast(I32), voc_words[0, :, 2 * GROUP : 2 * V].bitcast(I32))
         nc.sync.dma_start(offsets[:], offs)
-        sw_cols = sb.tile([P, 4], F32, name="sw_cols", tag="small0")
-        nc.sync.dma_start(sw_cols[:], sw.rearrange("o (p c) -> (o p) c", c=4))
+        sw_cols = sb.tile([P, 4], F32, name="sw_cols", tag="small")
+        nc.sync.dma_start(sw_cols[:], sw.rearrange("o (n c) -> (o n) c", c=4))
 
         codes, scales = [], []
         for name, raw, cast in (("hid", hid_raw, nc.vector.tensor_copy), ("dhid", dhid_raw, nc.scalar.copy)):
-            grouped = sb.tile([P, Q, 4], BF16, name=name + "_grouped", align_bytes=64)
+            grouped = sb.tile([P, Q, PACK], BF16, name=name + "_grouped", align_bytes=64)
             cast(
                 grouped[:].rearrange("p (c i) t -> p c t i", i=4),
                 raw[:].rearrange("p t (c i) -> p c t i", i=4),
             )
-            cd = sb.tile([P, Q], U32, name=name + "_codes", align_bytes=64)
-            sc = sb.tile([P, Q], U8, name=name + "_scales", align_bytes=64)
-            nc.vector.quantize_mx(out=cd[:].bitcast(FP8X4), scales=sc[:], in_=grouped[:].rearrange("p q t -> p (q t)"))
-            codes.append(cd)
-            scales.append(sc)
+            side_codes = sb.tile([P, Q], U32, name=name + "_codes", align_bytes=64)
+            side_scales = sb.tile([P, Q], U8, name=name + "_scales", align_bytes=64)
+            nc.vector.quantize_mx(
+                out=side_codes[:].bitcast(FP8X4),
+                scales=side_scales[:],
+                in_=grouped[:].rearrange("p q t -> p (q t)"),
+            )
+            codes.append(side_codes)
+            scales.append(side_scales)
 
         mult_col = sb.tile([P, 1], F32, name="mult_col", tag="hid_grouped", align_bytes=64)
         nc.sync.dma_start(mult_col[:], mult)
@@ -88,174 +113,163 @@ def tile_attend_hvfocal_heads_kernel(tc, hid, voc_words, voc_scales, mult, sw, d
         ta = sb.tile([P, V], F32, name="ta")
         group_max = sb.tile([P, GROUPS], F32, name="group_max")
 
-        def score(side, g):
-            acc = bank(4 * side + g, "score%d_%d" % (side, g))
-            h, c0 = divmod(g * BANK, HALF)
+        def product(side, g):
+            acc = bank(GROUPS * side + g, "product%d_%d" % (side, g))
+            words = words_head[:] if g == 0 else words_rest[:, 2 * GROUP * (g - 1) : 2 * GROUP * g]
             nc.tensor.matmul_mx(
                 out=acc[:],
                 lhsT=codes[side][:].bitcast(FP8X4),
                 lhsT_scale=scales[side][:],
-                rhs=words[h][:, 2 * c0 : 2 * (c0 + BANK)].bitcast(FP4X4),
-                rhs_scale=voc_sc[:, g * BANK : (g + 1) * BANK],
+                rhs=words.bitcast(FP4X4),
+                rhs_scale=voc_sc[:, group_cols(g)],
                 start=True,
                 stop=True,
             )
-            cols = slice(g * BANK, (g + 1) * BANK)
-            if side == 0:
-                nc.vector.tensor_scalar(a[:, cols], acc[:], 1.0, None, ALU.mult, ALU.max, accum_out=group_max[:, g : g + 1])
-            else:
-                nc.scalar.copy(ta[:, cols], acc[:])
+            return acc
 
-        for g in range(GROUPS):
-            score(0, g)
-            score(1, g)
+        def product_a(g):
+            acc = product(0, g)
+            nc.vector.tensor_scalar(
+                a[:, group_cols(g)], acc[:], 1.0, None, ALU.mult, ALU.max, accum_out=group_max[:, g : g + 1]
+            )
+
+        def product_ta(g):
+            nc.scalar.copy(ta[:, group_cols(g)], product(1, g)[:])
+
+        product_a(0)
+        product_ta(0)
+        product_a(1)
+        for g in range(2, GROUPS):
+            product_a(g)
+            product_ta(g - 1)
+        product_ta(GROUPS - 1)
 
         sw_ps = bank(0, "sw_ps")
-        sw_sum_ps = bank(1, "sw_sum_ps")
+        sw_fours_ps = bank(1, "sw_fours_ps")
         for c in range(4):
             spread = sw_cols[:, c : c + 1].to_broadcast([P, P])
-            nc.tensor.transpose(sw_ps[:, c * P : (c + 1) * P], spread, ident[:])
-            nc.tensor.matmul(sw_sum_ps[:, 0:P], spread, ident[:], start=c == 0, stop=c == 3, is_transpose=True)
+            nc.tensor.transpose(sw_ps[:, BLOCKS[c]], spread, ident[:])
+            nc.tensor.matmul(sw_fours_ps[:, 0:P], spread, ident[:], start=c == 0, stop=c == 3, is_transpose=True)
 
-        neg_max = col("neg_max")
-        nc.vector.tensor_reduce(neg_max[:], group_max[:], AX.X, ALU.max, negate=True)
-        a_listed = sb.tile([P, SLOTS], F32, name="a_listed")
-        ta_listed = sb.tile([P, SLOTS], F32, name="ta_listed")
+        neg_max = column("neg_max")
+        nc.vector.tensor_reduce(neg_max[:], group_max[:], AXIS.X, ALU.max, negate=True)
+        a_listed, ta_listed = slot_tile("a_listed"), slot_tile("ta_listed")
         nc.vector.tensor_copy(a_listed[:], a[:].indirect(offsets[:]))
         nc.vector.tensor_copy(ta_listed[:], ta[:].indirect(offsets[:]))
 
         p = [sb.tile([P, HALF], F32, name="p%d" % h) for h in range(2)]
         xp = [sb.tile([P, HALF], F32, name="xp%d" % h) for h in range(2)]
-        z_half = [col("z_half%d" % h) for h in range(2)]
-        xz_half = [col("xz_half%d" % h) for h in range(2)]
-        px = sb.tile([P, SLOTS], F32, name="px")
+        z_half = [column("z_half%d" % h) for h in range(2)]
+        xz_half = [column("xz_half%d" % h) for h in range(2)]
+        px = slot_tile("px")
+        z0_m2, lnz_m2, log_shift = column("z0_m2"), column("lnz_m2"), column("log_shift")
+        z, rz, tbar = column("z"), column("rz"), column("tbar")
         nc.scalar.activation(p[0][:], a[:, 0:HALF], ACT.Exp, bias=neg_max[:], accum_out=z_half[0][:])
         nc.scalar.activation(px[:], a_listed[:], ACT.Exp, bias=neg_max[:])
         nc.scalar.activation(p[1][:], a[:, HALF:V], ACT.Exp, bias=neg_max[:], accum_out=z_half[1][:])
-        z, rz, tbar = col("z"), col("rz"), col("tbar")
-        nc.scalar.activation(z[:], z_half[0][:], ACT.Identity, bias=z_half[1][:])
-        lnz_m2 = col("lnz_m2")
-        beta = col("beta")
-        nc.scalar.activation(lnz_m2[:], z[:], ACT.Ln, scale=exp_m2[:])
-        nc.scalar.activation(beta[:], lnz_m2[:], ACT.Identity, scale=-1.0, bias=neg_max[:])
+        nc.gpsimd.tensor_tensor(z0_m2[:], z_half[0][:], exp_m2[:], ALU.mult)
+        nc.gpsimd.tensor_tensor(z[:], z_half[0][:], z_half[1][:], ALU.add)
+        nc.scalar.activation(lnz_m2[:], z_half[1][:], ACT.Ln, scale=exp_m2[:], bias=z0_m2[:])
+        nc.scalar.activation(log_shift[:], lnz_m2[:], ACT.Identity, scale=-1.0, bias=neg_max[:])
 
+        scpx, weight, xe = slot_tile("scpx"), slot_tile("weight"), slot_tile("xe")
+        scpx_sum, weight_sum, xe_sum = column("scpx_sum"), column("weight_sum"), column("xe_sum")
         nc.vector.scalar_tensor_tensor(xp[0][:], ta[:, 0:HALF], 1.0, p[0][:], ALU.mult, ALU.mult, accum_out=xz_half[0][:])
-        su = sb.tile([P, SLOTS], F32, name="su")
-        w = sb.tile([P, SLOTS], F32, name="w")
-        xe = sb.tile([P, SLOTS], F32, name="xe")
-        su_sum, w_sum, xe_sum = col("su_sum"), col("w_sum"), col("xe_sum")
         nc.vector.scalar_tensor_tensor(
-            su[:].rearrange("p (n c) -> p n c", c=4),
+            scpx[:].rearrange("p (n c) -> p n c", c=4),
             px[:].rearrange("p (n c) -> p n c", c=4),
             mult_col[:],
             sw_ps[:].rearrange("p (c n) -> p n c", c=4),
             ALU.mult,
             ALU.mult,
-            accum_out=su_sum[:],
+            accum_out=scpx_sum[:],
         )
         nc.vector.reciprocal(rz[:], z[:])
         nc.vector.scalar_tensor_tensor(xp[1][:], ta[:, HALF:V], 1.0, p[1][:], ALU.mult, ALU.mult, accum_out=xz_half[1][:])
-        neg_rz, q2, neg_q2 = col("neg_rz"), col("q2"), col("neg_q2")
-        nc.scalar.activation(neg_rz[:], rz[:], ACT.Copy, scale=-64.0)
-        nc.scalar.activation(q2[:], rz[:], ACT.Square, scale=8.0)
-        nc.scalar.activation(neg_q2[:], q2[:], ACT.Copy, scale=-1.0)
-        sw_quads = sb.tile([P, P], F32, name="sw_quads")
-        s64_sum = col("s64_sum")
-        nc.scalar.activation(sw_quads[:], sw_sum_ps[:, 0:P], ACT.Copy, scale=neg_rz[:], accum_out=s64_sum[:])
+
+        xs_factor, rz2, neg_rz2, sw_term = column("xs_factor"), column("rz2"), column("neg_rz2"), column("sw_term")
+        nc.scalar.activation(xs_factor[:], rz[:], ACT.Copy, scale=-OUT_SCALE)
+        nc.scalar.activation(rz2[:], rz[:], ACT.Square, scale=OUT_SCALE**0.5)
+        nc.scalar.activation(neg_rz2[:], rz2[:], ACT.Copy, scale=-1.0)
+        sw_fours = sb.tile([P, P], F32, name="sw_fours")
+        nc.scalar.activation(sw_fours[:], sw_fours_ps[:, 0:P], ACT.Copy, scale=xs_factor[:], accum_out=sw_term[:])
 
         nc.vector.tensor_scalar(tbar[:], xz_half[0][:], xz_half[1][:], rz[:], ALU.add, ALU.mult)
-        nc.vector.scalar_tensor_tensor(w[:], a_listed[:], beta[:], su[:], ALU.add, ALU.mult, accum_out=w_sum[:])
-        nc.vector.scalar_tensor_tensor(xe[:], ta_listed[:], tbar[:], w[:], ALU.subtract, ALU.mult, accum_out=xe_sum[:])
-        nc.vector.tensor_copy(xs[:].indirect(offsets[:]), xe[:])
+        nc.vector.scalar_tensor_tensor(weight[:], a_listed[:], log_shift[:], scpx[:], ALU.add, ALU.mult, accum_out=weight_sum[:])
+        nc.vector.scalar_tensor_tensor(xe[:], ta_listed[:], tbar[:], weight[:], ALU.subtract, ALU.mult, accum_out=xe_sum[:])
+        nc.vector.tensor_copy(scattered[:].indirect(offsets[:]), xe[:])
 
-        neg_tbar = col("neg_tbar")
+        neg_tbar, dz_rest, dz64 = column("neg_tbar"), column("dz_rest"), column("dz64")
+        dz_tbar, xdz64 = column("dz_tbar"), column("xdz64")
         nc.scalar.activation(neg_tbar[:], tbar[:], ACT.Copy, scale=-1.0)
-        dz_rest, dz64, dz_tbar, xdz64 = col("dz_rest"), col("dz64"), col("dz_tbar"), col("xdz64")
-        nc.scalar.activation(dz_rest[:], su_sum[:], ACT.Identity, scale=neg_q2[:], bias=s64_sum[:])
-        nc.scalar.activation(dz64[:], w_sum[:], ACT.Identity, scale=q2[:], bias=dz_rest[:])
+        nc.scalar.activation(dz_rest[:], scpx_sum[:], ACT.Identity, scale=neg_rz2[:], bias=sw_term[:])
+        nc.scalar.activation(dz64[:], weight_sum[:], ACT.Identity, scale=rz2[:], bias=dz_rest[:])
         nc.scalar.activation(dz_tbar[:], dz64[:], ACT.Copy, scale=neg_tbar[:])
-        nc.scalar.activation(xdz64[:], xe_sum[:], ACT.Identity, scale=q2[:], bias=dz_tbar[:])
+        nc.scalar.activation(xdz64[:], xe_sum[:], ACT.Identity, scale=rz2[:], bias=dz_tbar[:])
 
-        def part(tiles, g):
-            h, c0 = divmod(g * BANK, HALF)
-            return tiles[h][:, c0 : c0 + BANK]
+        def scaled(name, halves, g, factor):
+            term = group_tile("%s%d" % (name, g))
+            nc.scalar.activation(term[:], group_of(halves, g), ACT.Copy, scale=factor[:])
+            return term
 
-        def turn_add(acc, src, start, stop):
-            for j in range(4):
-                blk = slice(j * P, (j + 1) * P)
-                nc.tensor.matmul(acc[:, blk], src[:, blk], ident[:], start=start and j == 0, stop=stop and j == 3, is_transpose=True)
+        g = GPSIMD_GROUP
+        p_term = scaled("p_term", p, g, xdz64)
+        xp_term, with_base = group_tile("gpsimd_xp_term"), group_tile("gpsimd_with_base")
+        gpsimd_dense = group_tile("gpsimd_dense", tag="partial")
+        nc.gpsimd.tensor_scalar(xp_term[:], group_of(xp, g), dz64[:], 0.0, ALU.mult, ALU.add)
+        nc.gpsimd.tensor_tensor(with_base[:], xp_term[:], group_of(base_sb, g), ALU.add)
+        nc.gpsimd.tensor_tensor(gpsimd_dense[:], with_base[:], p_term[:], ALU.add)
 
-        turned = {}
-        lin = {}
-        pooled = {}
+        def turn_into(acc, term, first, last):
+            for j, block in enumerate(BLOCKS):
+                nc.tensor.matmul(
+                    acc[:, block],
+                    term[:, block],
+                    ident[:],
+                    start=first and j == 0,
+                    stop=last and j == len(BLOCKS) - 1,
+                    is_transpose=True,
+                )
 
-        def linear(g):
-            lin[g] = sb.tile([P, BANK], F32, name="lin%d" % g)
-            nc.scalar.activation(lin[g][:], ta[:, g * BANK : (g + 1) * BANK], ACT.Identity, scale=dz64[:], bias=xdz64[:])
-
-        def pool_group(g):
-            q1 = sb.tile([P, BANK], F32, name="q1_%d" % g)
-            pooled[g] = sb.tile([P, BANK], F32, name="pooled%d" % g)
-            nc.gpsimd.tensor_tensor(q1[:], lin[g][:], part(p, g), ALU.mult)
-            nc.gpsimd.tensor_tensor(pooled[g][:], q1[:], part(base_sb, g), ALU.add)
-
-        back = {}
-
-        def pe_first(g):
+        def sum_turned(g):
             acc = bank(g, "turned%d" % g)
-            turn_add(acc, part(base_sb, g), True, False)
-            if MODES[g] == "X":
-                t1 = sb.tile([P, BANK], F32, name="xp_dz%d" % g)
-                nc.scalar.activation(t1[:], part(xp, g), ACT.Copy, scale=dz64[:])
-                turn_add(acc, t1[:], False, False)
-            t2 = sb.tile([P, BANK], F32, name="p_xdz%d" % g)
-            if MODES[g] == "U":
-                nc.gpsimd.tensor_tensor(t2[:], lin[g][:], part(p, g), ALU.mult)
-            else:
-                nc.scalar.activation(t2[:], part(p, g), ACT.Copy, scale=xdz64[:])
-            turn_add(acc, t2[:], False, True)
-            turned[g] = acc
+            turn_into(acc, group_of(base_sb, g), True, False)
+            turn_into(acc, scaled("xp_term", xp, g, dz64)[:], False, False)
+            turn_into(acc, scaled("p_term", p, g, xdz64)[:], False, True)
+            return acc
 
-        def pe_second(g):
-            t3 = sb.tile([P, BANK], F32, name="turned_sb%d" % g)
-            nc.scalar.copy(t3[:], turned[g][:])
-            acc = bank(4 + g, "back%d" % g)
-            for j in range(4):
-                blk = slice(j * P, (j + 1) * P)
-                nc.tensor.transpose(acc[:, blk], t3[:, blk], ident[:])
-            back[g] = acc
+        def turn_back(g, acc):
+            turned_sb = group_tile("turned_sb%d" % g)
+            nc.scalar.copy(turned_sb[:], acc[:])
+            dense = bank(GROUPS + g, "dense%d" % g)
+            for block in BLOCKS:
+                nc.tensor.transpose(dense[:, block], turned_sb[:, block], ident[:])
+            return dense
 
-        def finish(g):
-            cols = slice(g * BANK, (g + 1) * BANK)
-            res = sb.tile([P, BANK], F32, name="res%d" % g)
-            if MODES[g] == "Z":
-                r1 = sb.tile([P, BANK], F32, name="r1_%d" % g)
-                r2 = sb.tile([P, BANK], F32, name="r2_%d" % g)
-                nc.vector.scalar_tensor_tensor(r1[:], part(xp, g), dz64[:], part(base_sb, g), ALU.mult, ALU.add)
-                nc.vector.scalar_tensor_tensor(r2[:], part(p, g), xdz64[:], r1[:], ALU.mult, ALU.add)
-                nc.vector.scalar_tensor_tensor(res[:], xs[:, cols], neg_rz[:], r2[:], ALU.mult, ALU.add)
-            elif MODES[g] == "W":
-                nc.vector.scalar_tensor_tensor(res[:], xs[:, cols], neg_rz[:], pooled[g][:], ALU.mult, ALU.add)
-            elif MODES[g] == "Y":
-                r1 = sb.tile([P, BANK], F32, name="r1_%d" % g)
-                nc.vector.scalar_tensor_tensor(r1[:], part(xp, g), dz64[:], back[g][:], ALU.mult, ALU.add)
-                nc.vector.scalar_tensor_tensor(res[:], xs[:, cols], neg_rz[:], r1[:], ALU.mult, ALU.add)
-            else:
-                nc.vector.scalar_tensor_tensor(res[:], xs[:, cols], neg_rz[:], back[g][:], ALU.mult, ALU.add)
-            nc.sync.dma_start(out[:, cols], res[:])
+        turned = [sum_turned(g) for g in TENSOR_GROUPS]
+        tensor_dense = [turn_back(g, acc) for g, acc in zip(TENSOR_GROUPS, turned)]
 
-        for g in range(GROUPS):
-            if MODES[g] in ("W", "U"):
-                linear(g)
-        for g in range(GROUPS):
-            if MODES[g] == "W":
-                pool_group(g)
-        pe_groups = [g for g in range(GROUPS) if MODES[g] in ("X", "Y", "U")]
-        for k, g in enumerate(pe_groups):
-            pe_first(g)
-            if k > 0:
-                pe_second(pe_groups[k - 1])
-        if pe_groups:
-            pe_second(pe_groups[-1])
-        for g in range(GROUPS):
-            finish(g)
+        def add_scattered_and_store(g, dense, pieces):
+            result = group_tile("result%d" % g)
+            for piece in pieces:
+                cols = slice(g * GROUP + piece.start, g * GROUP + piece.stop)
+                nc.vector.scalar_tensor_tensor(result[:, piece], scattered[:, cols], xs_factor[:], dense[:, piece], ALU.mult, ALU.add)
+                nc.sync.dma_start(out[:, cols], result[:, piece])
+
+        whole = [slice(0, GROUP)]
+        add_scattered_and_store(GPSIMD_GROUP, gpsimd_dense, whole)
+
+        g = VECTOR_GROUP
+        with_scattered, with_xp, result = group_tile("with_scattered", tag="partial"), group_tile("with_xp"), group_tile("result%d" % g)
+        steps = (
+            (with_scattered[:], scattered[:, group_cols(g)], xs_factor, group_of(base_sb, g)),
+            (with_xp[:], group_of(xp, g), dz64, with_scattered[:]),
+            (result[:], group_of(p, g), xdz64, with_xp[:]),
+        )
+        for total, term, factor, so_far in steps:
+            for piece in GROUP_HALVES:
+                nc.vector.scalar_tensor_tensor(total[:, piece], term[:, piece], factor[:], so_far[:, piece], ALU.mult, ALU.add)
+        nc.sync.dma_start(out[:, group_cols(g)], result[:])
+
+        add_scattered_and_store(TENSOR_GROUPS[0], tensor_dense[0], whole)
+        add_scattered_and_store(TENSOR_GROUPS[1], tensor_dense[1], GROUP_HALVES)

from contextlib import ExitStack

import concourse.mybir as mybir
from concourse.masks import make_identity

F32 = mybir.dt.float32
BF16 = mybir.dt.bfloat16
I32 = mybir.dt.int32
U32 = mybir.dt.uint32
U16 = mybir.dt.uint16
U8 = mybir.dt.uint8
FP8X4 = mybir.dt.float8_e4m3fn_x4
FP4X4 = mybir.dt.float4_e2m1fn_x4
ALU = mybir.AluOpType
ACT = mybir.ActivationFunctionType
AXIS = mybir.AxisListType

P = 128
PACK = 4
D, V, Q, SLOTS = 512, 2048, 128, 512
GROUP = 512
GROUPS = V // GROUP
HALF = V // 2
BLOCKS = [slice(j * P, (j + 1) * P) for j in range(GROUP // P)]
GROUP_HALVES = [slice(0, GROUP // 2), slice(GROUP // 2, GROUP)]
OUT_SCALE = 64.0

GPSIMD_GROUP = 0
VECTOR_GROUP = 1
TENSOR_GROUPS = (2, 3)

FLOPS = 2 * 2 * D * V * Q


def tile_attend_hvfocal_heads_kernel(tc, hid, voc_words, voc_scales, mult, sw, dhid, base, offs, out):
    nc = tc.nc
    with ExitStack() as ctx:
        sb = ctx.enter_context(tc.tile_pool(name="sb", bufs=1))
        ps = ctx.enter_context(tc.psum_pool(name="ps", bufs=1))

        def column(name):
            return sb.tile([P, 1], F32, name=name)

        def slot_tile(name):
            return sb.tile([P, SLOTS], F32, name=name)

        def group_tile(name, tag=None):
            return sb.tile([P, GROUP], F32, name=name, tag=tag or name)

        def bank(b, name):
            return ps.tile([P, GROUP], F32, name=name, tag="bank%d" % b)

        def group_cols(g):
            return slice(g * GROUP, (g + 1) * GROUP)

        def group_of(halves, g):
            h, c0 = divmod(g * GROUP, HALF)
            return halves[h][:, c0 : c0 + GROUP]

        offsets = sb.tile([P, SLOTS // 16], U16, name="offsets")
        voc_sc = sb.tile([P, V], U8, name="voc_sc", align_bytes=64)
        scattered = sb.tile([P, V], F32, name="scattered")
        minus_two = sb.tile([P, 1], F32, name="minus_two", tag="small")
        nc.vector.memset(voc_sc[:].bitcast(I32), 0)
        nc.vector.memset(minus_two[:], -2.0)
        nc.vector.memset(scattered[:], 0.0)
        ident = sb.tile([P, P], F32, name="ident")
        make_identity(nc, ident[:])
        exp_m2 = column("exp_m2")
        nc.scalar.activation(exp_m2[:], minus_two[:], ACT.Exp)

        hid_raw = sb.tile([P, PACK, Q], F32, name="hid_raw", tag="raw0")
        dhid_raw = sb.tile([P, PACK, Q], F32, name="dhid_raw", tag="raw1")
        words_head = sb.tile([P, 2 * GROUP], U8, name="words_head", align_bytes=64)
        words_rest = sb.tile([P, 2 * (V - GROUP)], U8, name="words_rest", align_bytes=64)
        nc.sync.dma_start(hid_raw[:], hid.rearrange("(p t) q -> p t q", t=PACK))
        for quad in range(4):
            nc.sync.dma_start(
                voc_sc[32 * quad : 32 * quad + 4, :].bitcast(I32),
                voc_scales[0, 4 * quad : 4 * quad + 4, :].bitcast(I32),
            )
        nc.sync.dma_start(words_head[:].bitcast(I32), voc_words[0, :, 0 : 2 * GROUP].bitcast(I32))
        nc.sync.dma_start(dhid_raw[:], dhid.rearrange("(p t) q -> p t q", t=PACK))
        nc.sync.dma_start(words_rest[:].bitcast(I32), voc_words[0, :, 2 * GROUP : 2 * V].bitcast(I32))
        nc.sync.dma_start(offsets[:], offs)
        sw_cols = sb.tile([P, 4], F32, name="sw_cols", tag="small")
        nc.sync.dma_start(sw_cols[:], sw.rearrange("o (n c) -> (o n) c", c=4))

        codes, scales = [], []
        for name, raw, cast in (("hid", hid_raw, nc.vector.tensor_copy), ("dhid", dhid_raw, nc.scalar.copy)):
            grouped = sb.tile([P, Q, PACK], BF16, name=name + "_grouped", align_bytes=64)
            cast(
                grouped[:].rearrange("p (c i) t -> p c t i", i=4),
                raw[:].rearrange("p t (c i) -> p c t i", i=4),
            )
            side_codes = sb.tile([P, Q], U32, name=name + "_codes", align_bytes=64)
            side_scales = sb.tile([P, Q], U8, name=name + "_scales", align_bytes=64)
            nc.vector.quantize_mx(
                out=side_codes[:].bitcast(FP8X4),
                scales=side_scales[:],
                in_=grouped[:].rearrange("p q t -> p (q t)"),
            )
            codes.append(side_codes)
            scales.append(side_scales)

        mult_col = sb.tile([P, 1], F32, name="mult_col", tag="hid_grouped", align_bytes=64)
        nc.sync.dma_start(mult_col[:], mult)
        base_sb = [sb.tile([P, HALF], F32, name="base%d" % h, tag="raw%d" % h) for h in range(2)]
        for h in range(2):
            nc.sync.dma_start(base_sb[h][:], base[:, h * HALF : (h + 1) * HALF])

        a = sb.tile([P, V], F32, name="a")
        ta = sb.tile([P, V], F32, name="ta")
        group_max = sb.tile([P, GROUPS], F32, name="group_max")

        def product(side, g):
            acc = bank(GROUPS * side + g, "product%d_%d" % (side, g))
            words = words_head[:] if g == 0 else words_rest[:, 2 * GROUP * (g - 1) : 2 * GROUP * g]
            nc.tensor.matmul_mx(
                out=acc[:],
                lhsT=codes[side][:].bitcast(FP8X4),
                lhsT_scale=scales[side][:],
                rhs=words.bitcast(FP4X4),
                rhs_scale=voc_sc[:, group_cols(g)],
                start=True,
                stop=True,
            )
            return acc

        def product_a(g):
            acc = product(0, g)
            nc.vector.tensor_scalar(
                a[:, group_cols(g)], acc[:], 1.0, None, ALU.mult, ALU.max, accum_out=group_max[:, g : g + 1]
            )

        def product_ta(g):
            nc.scalar.copy(ta[:, group_cols(g)], product(1, g)[:])

        product_a(0)
        product_ta(0)
        product_a(1)
        for g in range(2, GROUPS):
            product_a(g)
            product_ta(g - 1)
        product_ta(GROUPS - 1)

        sw_ps = bank(0, "sw_ps")
        sw_fours_ps = bank(1, "sw_fours_ps")
        for c in range(4):
            spread = sw_cols[:, c : c + 1].to_broadcast([P, P])
            nc.tensor.transpose(sw_ps[:, BLOCKS[c]], spread, ident[:])
            nc.tensor.matmul(sw_fours_ps[:, 0:P], spread, ident[:], start=c == 0, stop=c == 3, is_transpose=True)

        neg_max = column("neg_max")
        nc.vector.tensor_reduce(neg_max[:], group_max[:], AXIS.X, ALU.max, negate=True)
        a_listed, ta_listed = slot_tile("a_listed"), slot_tile("ta_listed")
        nc.vector.tensor_copy(a_listed[:], a[:].indirect(offsets[:]))
        nc.vector.tensor_copy(ta_listed[:], ta[:].indirect(offsets[:]))

        p = [sb.tile([P, HALF], F32, name="p%d" % h) for h in range(2)]
        xp = [sb.tile([P, HALF], F32, name="xp%d" % h) for h in range(2)]
        z_half = [column("z_half%d" % h) for h in range(2)]
        xz_half = [column("xz_half%d" % h) for h in range(2)]
        px = slot_tile("px")
        z0_m2, lnz_m2, log_shift = column("z0_m2"), column("lnz_m2"), column("log_shift")
        z, rz, tbar = column("z"), column("rz"), column("tbar")
        nc.scalar.activation(p[0][:], a[:, 0:HALF], ACT.Exp, bias=neg_max[:], accum_out=z_half[0][:])
        nc.scalar.activation(px[:], a_listed[:], ACT.Exp, bias=neg_max[:])
        nc.scalar.activation(p[1][:], a[:, HALF:V], ACT.Exp, bias=neg_max[:], accum_out=z_half[1][:])
        nc.gpsimd.tensor_tensor(z0_m2[:], z_half[0][:], exp_m2[:], ALU.mult)
        nc.gpsimd.tensor_tensor(z[:], z_half[0][:], z_half[1][:], ALU.add)
        nc.scalar.activation(lnz_m2[:], z_half[1][:], ACT.Ln, scale=exp_m2[:], bias=z0_m2[:])
        nc.scalar.activation(log_shift[:], lnz_m2[:], ACT.Identity, scale=-1.0, bias=neg_max[:])

        scpx, weight, xe = slot_tile("scpx"), slot_tile("weight"), slot_tile("xe")
        scpx_sum, weight_sum, xe_sum = column("scpx_sum"), column("weight_sum"), column("xe_sum")
        nc.vector.scalar_tensor_tensor(xp[0][:], ta[:, 0:HALF], 1.0, p[0][:], ALU.mult, ALU.mult, accum_out=xz_half[0][:])
        nc.vector.scalar_tensor_tensor(
            scpx[:].rearrange("p (n c) -> p n c", c=4),
            px[:].rearrange("p (n c) -> p n c", c=4),
            mult_col[:],
            sw_ps[:].rearrange("p (c n) -> p n c", c=4),
            ALU.mult,
            ALU.mult,
            accum_out=scpx_sum[:],
        )
        nc.vector.reciprocal(rz[:], z[:])
        nc.vector.scalar_tensor_tensor(xp[1][:], ta[:, HALF:V], 1.0, p[1][:], ALU.mult, ALU.mult, accum_out=xz_half[1][:])

        xs_factor, rz2, neg_rz2, sw_term = column("xs_factor"), column("rz2"), column("neg_rz2"), column("sw_term")
        nc.scalar.activation(xs_factor[:], rz[:], ACT.Copy, scale=-OUT_SCALE)
        nc.scalar.activation(rz2[:], rz[:], ACT.Square, scale=OUT_SCALE**0.5)
        nc.scalar.activation(neg_rz2[:], rz2[:], ACT.Copy, scale=-1.0)
        sw_fours = sb.tile([P, P], F32, name="sw_fours")
        nc.scalar.activation(sw_fours[:], sw_fours_ps[:, 0:P], ACT.Copy, scale=xs_factor[:], accum_out=sw_term[:])

        nc.vector.tensor_scalar(tbar[:], xz_half[0][:], xz_half[1][:], rz[:], ALU.add, ALU.mult)
        nc.vector.scalar_tensor_tensor(weight[:], a_listed[:], log_shift[:], scpx[:], ALU.add, ALU.mult, accum_out=weight_sum[:])
        nc.vector.scalar_tensor_tensor(xe[:], ta_listed[:], tbar[:], weight[:], ALU.subtract, ALU.mult, accum_out=xe_sum[:])
        nc.vector.tensor_copy(scattered[:].indirect(offsets[:]), xe[:])

        neg_tbar, dz_rest, dz64 = column("neg_tbar"), column("dz_rest"), column("dz64")
        dz_tbar, xdz64 = column("dz_tbar"), column("xdz64")
        nc.scalar.activation(neg_tbar[:], tbar[:], ACT.Copy, scale=-1.0)
        nc.scalar.activation(dz_rest[:], scpx_sum[:], ACT.Identity, scale=neg_rz2[:], bias=sw_term[:])
        nc.scalar.activation(dz64[:], weight_sum[:], ACT.Identity, scale=rz2[:], bias=dz_rest[:])
        nc.scalar.activation(dz_tbar[:], dz64[:], ACT.Copy, scale=neg_tbar[:])
        nc.scalar.activation(xdz64[:], xe_sum[:], ACT.Identity, scale=rz2[:], bias=dz_tbar[:])

        def scaled(name, halves, g, factor):
            term = group_tile("%s%d" % (name, g))
            nc.scalar.activation(term[:], group_of(halves, g), ACT.Copy, scale=factor[:])
            return term

        g = GPSIMD_GROUP
        p_term = scaled("p_term", p, g, xdz64)
        xp_term, with_base = group_tile("gpsimd_xp_term"), group_tile("gpsimd_with_base")
        gpsimd_dense = group_tile("gpsimd_dense", tag="partial")
        nc.gpsimd.tensor_scalar(xp_term[:], group_of(xp, g), dz64[:], 0.0, ALU.mult, ALU.add)
        nc.gpsimd.tensor_tensor(with_base[:], xp_term[:], group_of(base_sb, g), ALU.add)
        nc.gpsimd.tensor_tensor(gpsimd_dense[:], with_base[:], p_term[:], ALU.add)

        def turn_into(acc, term, first, last):
            for j, block in enumerate(BLOCKS):
                nc.tensor.matmul(
                    acc[:, block],
                    term[:, block],
                    ident[:],
                    start=first and j == 0,
                    stop=last and j == len(BLOCKS) - 1,
                    is_transpose=True,
                )

        def sum_turned(g):
            acc = bank(g, "turned%d" % g)
            turn_into(acc, group_of(base_sb, g), True, False)
            turn_into(acc, scaled("xp_term", xp, g, dz64)[:], False, False)
            turn_into(acc, scaled("p_term", p, g, xdz64)[:], False, True)
            return acc

        def turn_back(g, acc):
            turned_sb = group_tile("turned_sb%d" % g)
            nc.scalar.copy(turned_sb[:], acc[:])
            dense = bank(GROUPS + g, "dense%d" % g)
            for block in BLOCKS:
                nc.tensor.transpose(dense[:, block], turned_sb[:, block], ident[:])
            return dense

        turned = [sum_turned(g) for g in TENSOR_GROUPS]
        tensor_dense = [turn_back(g, acc) for g, acc in zip(TENSOR_GROUPS, turned)]

        def add_scattered_and_store(g, dense, pieces):
            result = group_tile("result%d" % g)
            for piece in pieces:
                cols = slice(g * GROUP + piece.start, g * GROUP + piece.stop)
                nc.vector.scalar_tensor_tensor(result[:, piece], scattered[:, cols], xs_factor[:], dense[:, piece], ALU.mult, ALU.add)
                nc.sync.dma_start(out[:, cols], result[:, piece])

        whole = [slice(0, GROUP)]
        add_scattered_and_store(GPSIMD_GROUP, gpsimd_dense, whole)

        g = VECTOR_GROUP
        with_scattered, with_xp, result = group_tile("with_scattered", tag="partial"), group_tile("with_xp"), group_tile("result%d" % g)
        steps = (
            (with_scattered[:], scattered[:, group_cols(g)], xs_factor, group_of(base_sb, g)),
            (with_xp[:], group_of(xp, g), dz64, with_scattered[:]),
            (result[:], group_of(p, g), xdz64, with_xp[:]),
        )
        for total, term, factor, so_far in steps:
            for piece in GROUP_HALVES:
                nc.vector.scalar_tensor_tensor(total[:, piece], term[:, piece], factor[:], so_far[:, piece], ALU.mult, ALU.add)
        nc.sync.dma_start(out[:, group_cols(g)], result[:])

        add_scattered_and_store(TENSOR_GROUPS[0], tensor_dense[0], whole)
        add_scattered_and_store(TENSOR_GROUPS[1], tensor_dense[1], GROUP_HALVES)
